import numpy as np
import ml_dtypes


def mxq(x, axis, fmt="e4m3"):
    dtype, down = {"e4m3": (ml_dtypes.float8_e4m3fn, 7), "e5m2": (ml_dtypes.float8_e5m2, 14)}[fmt]
    v = np.moveaxis(np.asarray(x, np.float32).astype(ml_dtypes.bfloat16).astype(np.float64), axis, -1)
    blocks = v.reshape(v.shape[:-1] + (-1, 32))
    amax = np.abs(blocks).max(-1, keepdims=True)
    byte = np.maximum(np.where(amax > 0, np.frexp(amax)[1] - 1 + 127, 0) - down, 1)
    scale = np.exp2(byte - 127.0)
    codes = (blocks / scale).astype(np.float32).astype(dtype).astype(np.float64)
    return np.moveaxis((codes * scale).reshape(v.shape), -1, axis)


WIDE = False


def mx_kscale(k):
    if not WIDE:
        return np.ones(k)
    levels = np.array([10, -10, 5, -5, 0])
    if k % 512:
        return np.exp2(np.random.permutation(np.resize(levels, k // 32))).repeat(32)
    a = np.empty((k // 512, 16))
    for p in range(k // 512):
        a[p, :8] = np.random.permutation(np.resize(levels, 8))
        for g in range(8):
            far = levels[np.abs(levels - a[p, g]) >= 10]
            a[p, g + 8] = far[np.random.randint(len(far))]
    return np.exp2(a.ravel()).repeat(32)


def f64(x):
    return np.asarray(x).astype(np.float64)


def striped(idx):
    return np.tile(np.asarray(idx).reshape(-1, 16).T, (8, 1)).astype(np.uint16)


def unstriped(offs):
    return offs[:16].T.reshape(-1).astype(np.int64)


E2M1 = np.array([0.0, 0.5, 1.0, 1.5, 2.0, 3.0, 4.0, 6.0, -0.0, -0.5, -1.0, -1.5, -2.0, -3.0, -4.0, -6.0])


def pack_weight(w, fmt):
    k, n = w.shape
    w = f64(np.asarray(w, np.float32).astype(ml_dtypes.bfloat16)).reshape(k // 32, 32, n)
    amax = np.abs(w).max(1)
    if fmt == "e4m3":
        byte = np.frexp(amax)[1] - 1 + 127 - 7
    else:
        mant, ex = np.frexp(amax / 6.0)
        byte = np.where(mant > 0.5, ex, ex - 1) + 127
    byte = np.clip(np.where(amax > 0, byte, 1), 1, 254)
    scaled = (w * np.exp2(127.0 - byte)[:, None, :]).reshape(k, n).astype(np.float32)
    by_word = np.ascontiguousarray(scaled.reshape(k // 512, 128, 4, n).transpose(0, 1, 3, 2))
    if fmt == "e4m3":
        words = by_word.astype(ml_dtypes.float8_e4m3fn).view(np.uint8)
    else:
        c = by_word.astype(ml_dtypes.float4_e2m1fn).view(np.uint8) & 0xF
        words = (c[..., 0::2] | (c[..., 1::2] << 4)).reshape(k // 512, 128, 2 * n)
    return np.ascontiguousarray(words), np.ascontiguousarray(byte.astype(np.uint8).reshape(k // 512, 16, n))


def unpack_weight(words, scales, fmt):
    g, _, n = scales.shape
    words = np.ascontiguousarray(words).reshape(g, 128, n, -1)
    if fmt == "e4m3":
        vals = words.view(ml_dtypes.float8_e4m3fn).astype(np.float64)
    else:
        nib = np.empty((g, 128, n, 4), np.uint8)
        nib[..., 0::2] = words & 0xF
        nib[..., 1::2] = words >> 4
        vals = E2M1[nib]
    vals = vals * np.repeat(np.exp2(scales.astype(np.float64) - 127.0), 8, axis=1)[..., None]
    return vals.transpose(0, 1, 3, 2).reshape(g * 512, n)


def silu(v):
    return v / (1.0 + np.exp(-v))


K, T, J, N = 1024, 2048, 512, 512


def setup_inputs():
    n = np.random.standard_normal
    idx = np.random.permutation(T)[:J]
    fk = mx_kscale(K)
    xqp = pack_weight(n((K, T)) / fk[:, None], "e4m3")
    wbp = pack_weight(n((K, N)) * 1 / np.sqrt(K) * fk[:, None], "e2m1")
    return {
        "xq_words": xqp[0],
        "xq_scales": xqp[1],
        "wa": (n((K, N)) * 1 / np.sqrt(K) * fk[:, None]).astype(np.float32),
        "wb_words": wbp[0],
        "wb_scales": wbp[1],
        "ga": (np.random.uniform(0.4, 1.2, (1, J))).astype(np.float32),
        "offs": striped(idx),
    }


def reference(xq_words, xq_scales, wa, wb_words, wb_scales, ga, offs):
    idx = unstriped(offs)
    xqu = unpack_weight(xq_words, xq_scales, "e4m3")
    wbu = unpack_weight(wb_words, wb_scales, "e2m1")
    waq = mxq(f64(wa), 0, "e4m3")
    xqidxg = xqu[:, idx]
    p = waq.T @ xqidxg
    q = wbu.T @ xqidxg
    qs = np.pad(q, ((0, 0), (1, 0)))[:, :J]
    y = silu(p + f64(ga) * qs)
    return y

@@ -1,0 +1,202 @@
+from contextlib import ExitStack
+
+import concourse.mybir as mybir
+
+K, T, J, N = 1024, 2048, 512, 512
+FLOPS = 2 * 2 * K * N * J
+
+F32 = mybir.dt.float32
+BF16 = mybir.dt.bfloat16
+I32 = mybir.dt.int32
+U32 = mybir.dt.uint32
+U16 = mybir.dt.uint16
+U8 = mybir.dt.uint8
+FP8X4 = mybir.dt.float8_e4m3fn_x4
+FP4X4 = mybir.dt.float4_e2m1fn_x4
+MULT = mybir.AluOpType.mult
+ADD = mybir.AluOpType.add
+SILU = mybir.ActivationFunctionType.Silu
+
+P = 128
+PACK = 4
+PASSES = 2
+TILES = N // P
+HALF = N // 2
+LIFT = 16
+
+
+def tile_list_expert_and_neighbour_kernel(tc, xq_words, xq_scales, wa, wb_words, wb_scales, ga, offs, out):
+    nc = tc.nc
+    with ExitStack() as ctx:
+        keep = ctx.enter_context(tc.tile_pool(name="keep", bufs=1))
+        placed = ctx.enter_context(tc.tile_pool(name="placed", bufs=1))
+        psum = ctx.enter_context(tc.psum_pool(name="psum", bufs=1))
+
+        offsets = keep.tile([P, J // 16], U16, name="offsets")
+        blank = placed.tile([P, 3 * P], F32, name="blank", align_bytes=64, offset=7936)
+        xs_table = placed.tile([P, T], U8, name="xs_table", align_bytes=64, offset=11264+0)
+        x_table = [
+            keep.tile([P, T], I32, name="x_table0", align_bytes=64),
+            placed.tile([P, T], I32, name="x_table1", align_bytes=64, offset=0),
+        ]
+        wb_codes = [
+            keep.tile([P, 2 * N], U8, name="wb_codes0", align_bytes=64),
+            placed.tile([P, 2 * N], U8, name="wb_codes1", align_bytes=64, offset=9216),
+        ]
+        x_codes = [
+            placed.tile([P, J], U32, name="x_codes0", align_bytes=64, offset=10240),
+            keep.tile([P, J], U32, name="x_codes1", align_bytes=64),
+        ]
+        wa_raw = placed.tile([P, PASSES * PACK * N], F32, name="wa_raw", align_bytes=64, offset=12288)
+        xs_picked = keep.tile([P, J], U8, name="xs_picked", align_bytes=64)
+        xs_lowered = keep.tile([P, J], U8, name="xs_lowered", align_bytes=64)
+        x_scales = [xs_picked, xs_lowered]
+        wb_planes = placed.tile([P, PASSES, N], U8, name="wb_planes", align_bytes=64, offset=8192)
+        ga_rows = keep.tile([P, PACK], F32, name="ga_rows")
+        ga_wide = placed.tile([P, J], F32, name="ga_wide", align_bytes=64, offset=28672)
+        identity = keep.tile([P, P], F32, name="identity")
+        zero = keep.tile([P, 1], F32, name="zero")
+        wa_first = wa_raw[:, 0 : PACK * N].rearrange("p (j n) -> p j n", j=PACK)
+        wa_second = [
+            wa_raw[:, PACK * (N + HALF * h) : PACK * (N + HALF * (h + 1))].rearrange("p (j n) -> p j n", j=PACK)
+            for h in range(2)
+        ]
+        wa_bf = [[keep.tile([P, HALF * PACK], BF16, name=f"wa_bf0{h}", align_bytes=64) for h in range(2)]]
+        wa_bf.append([
+            placed.tile([P, HALF * PACK], BF16, name="wa_bf10", align_bytes=64, offset=28672 + 1024),
+            keep.tile([P, HALF * PACK], BF16, name="wa_bf11", align_bytes=64),
+        ])
+        wa_codes = [[keep.tile([P, HALF], U32, name=f"wa_codes{z}{h}", align_bytes=64) for h in range(2)] for z in range(PASSES)]
+        last_codes = placed.tile([P, P], U32, name="last_codes", align_bytes=64, offset=32768)
+        wa_planes = [[placed.tile([P, HALF], U8, name=f"wa_planes{z}{h}", align_bytes=64, offset=28672 + HALF * (2 * z + h)) for h in range(2)] for z in range(PASSES)]
+        message = [placed.tile([P, J], F32, name=f"message{i}", align_bytes=64, offset=32768 + 4 * J * ((i - 0) % TILES)) for i in range(TILES)]
+        summed = [keep.tile([P, J], F32, name=f"summed{i}") for i in range(TILES)]
+        result = [keep.tile([P, J], F32, name=f"result{i}") for i in range(TILES)]
+        q_bank = [psum.tile([P, J], F32, name=f"q_bank{i}") for i in range(TILES)]
+        p_bank = [psum.tile([P, J], F32, name=f"p_bank{i}") for i in range(TILES)]
+
+        nc.gpsimd.memset(xs_table[:].bitcast(I32), 0)
+        nc.gpsimd.memset(blank[:, 0:P], 0.0)
+        nc.gpsimd.affine_select(
+            out=identity[:], in_=blank[:, 0:P], compare_op=mybir.AluOpType.not_equal, fill=1.0, base=0,
+            pattern=[[-1, P]], channel_multiplier=1,
+        )
+        nc.gpsimd.memset(wb_planes[:].rearrange("p z n -> p (z n)").bitcast(I32), 0)
+        nc.vector.memset(xs_lowered[:].bitcast(I32), 0)
+        nc.vector.memset(zero[:], 0.0)
+
+        nc.sync.dma_start(offsets[:], offs)
+        nc.sync.dma_start(x_table[0][:], xq_words[0].rearrange("p t b -> p (t b)").bitcast(I32))
+        nc.sync.dma_start(wb_codes[0][:].bitcast(I32), wb_words[0].bitcast(I32))
+        nc.scalar.dma_start(ga_rows[:], ga.rearrange("o (p t) -> (o p) t", t=PACK))
+        xs_rows = xq_scales.rearrange("z (q r) t -> r q z t", r=4)
+        for r in range(4):
+            nc.sync.dma_start(xs_table[r:P:LIFT, :].bitcast(I32), xs_rows[r].bitcast(I32))
+        nc.sync.dma_start(x_table[1][:], xq_words[1].rearrange("p t b -> p (t b)").bitcast(I32))
+        nc.sync.dma_start(wb_codes[1][:].bitcast(I32), wb_words[1].bitcast(I32))
+        for q in range(4):
+            nc.sync.dma_start(
+                wb_planes[32 * q : 32 * q + 4, :, :].bitcast(I32),
+                wb_scales[:, 4 * q : 4 * q + 4, :].rearrange("z r n -> r z n").bitcast(I32),
+            )
+
+        for i in range(TILES):
+            nc.scalar.activation(message[i][:, 0:1], zero[:], SILU)
+
+        nc.vector.tensor_copy(xs_picked[:], xs_table[:].indirect(offsets[:]))
+        nc.sync.dma_start(xs_lowered[0 : P - LIFT, :].bitcast(I32), xs_picked[LIFT:P, :].bitcast(I32))
+        for u in range(2):
+            nc.sync.dma_start(wa_first[:, 2 * u : 2 * u + 2, :], wa[0:512, :].rearrange("(p j) n -> p j n", j=PACK)[:, 2 * u : 2 * u + 2, :])
+        for h in range(2):
+            nc.sync.dma_start(
+                wa_second[h], wa[512:1024, h * HALF : (h + 1) * HALF].rearrange("(p j) n -> p j n", j=PACK)
+            )
+
+        spread = p_bank[TILES - 1][:].rearrange("n (t p) -> n t p", t=PACK)
+        for t in range(PACK):
+            nc.tensor.transpose(spread[:, t, :], ga_rows[:, t : t + 1].to_broadcast([P, P]), identity[:])
+        nc.scalar.copy(ga_wide[:].rearrange("n (p t) -> n p t", t=PACK), spread.rearrange("n t p -> n p t"))
+
+        for z in range(PASSES):
+            nc.vector.tensor_copy(x_codes[z][:], x_table[z][:].bitcast(U32).indirect(offsets[:]))
+            for i in range(TILES):
+                nc.tensor.matmul_mx(
+                    out=q_bank[i][:],
+                    lhsT=wb_codes[z][:, 2 * P * i : 2 * P * (i + 1)].bitcast(FP4X4),
+                    lhsT_scale=wb_planes[:, z, P * i : P * (i + 1)],
+                    rhs=x_codes[z][:].bitcast(FP8X4),
+                    rhs_scale=x_scales[z][:],
+                    start=(z == 0),
+                    stop=(z == PASSES - 1),
+                )
+
+        def pool_copy(dst, src):
+            nc.gpsimd.tensor_scalar(dst, src, 1.0, 0.0, MULT, ADD)
+
+        S, V, G = nc.scalar.copy, nc.vector.tensor_copy, pool_copy
+
+        def weave(engine_copy, z, i, count=1):
+            h, c = divmod(i, 2)
+            rows = wa_first[:, :, P * i : P * (i + count)] if z == 0 else wa_second[h][:, :, P * c : P * (c + count)]
+            dst = wa_bf[z][h][:, PACK * P * c : PACK * P * (c + count)]
+            engine_copy(
+                dst.rearrange("p (c i t) -> p c t i", i=4, t=PACK), rows.rearrange("p t (c i) -> p c t i", i=4)
+            )
+
+        def codes(z, h, c0, c1):
+            return last_codes[:] if (z, h, c0) == (1, 1, 1) else wa_codes[z][h][:, P * c0 : P * c1]
+
+        def quantize(z, h, c0, c1):
+            nc.vector.quantize_mx(
+                out=codes(z, h, c0, c1).bitcast(FP8X4),
+                scales=wa_planes[z][h][:, P * c0 : P * c1],
+                in_=wa_bf[z][h][:, PACK * P * c0 : PACK * P * c1],
+            )
+
+        def own_pass(z, i):
+            h, c = divmod(i, 2)
+            nc.tensor.matmul_mx(
+                out=p_bank[i][:],
+                lhsT=codes(z, h, c, c + 1).bitcast(FP8X4),
+                lhsT_scale=wa_planes[z][h][:, P * c : P * (c + 1)],
+                rhs=x_codes[z][:].bitcast(FP8X4),
+                rhs_scale=x_scales[z][:],
+                start=(z == 0),
+                stop=(z == PASSES - 1),
+            )
+
+        def weigh(i):
+            nc.vector.tensor_tensor(message[i][:, 1:J], q_bank[i][:, 0 : J - 1], ga_wide[:, 1:J], MULT)
+
+        def finish(i, parts=1):
+            w = J // parts
+            for s in range(parts):
+                cols = slice(w * s, w * (s + 1))
+                nc.vector.tensor_tensor(summed[i][:, cols], p_bank[i][:, cols], message[i][:, cols], ADD)
+                nc.scalar.activation(result[i][:, cols], summed[i][:, cols], SILU)
+                nc.sync.dma_start(out[P * i : P * (i + 1), cols], result[i][:, cols])
+
+        for i in range(TILES):
+            weigh(i)
+        weave(S, 0, 0, 2)
+        weave(S, 0, 2, 2)
+        quantize(0, 0, 0, 2)
+        own_pass(0, 0)
+        own_pass(0, 1)
+        weave(V, 1, 0, 2)
+        quantize(0, 1, 0, 2)
+        own_pass(0, 2)
+        own_pass(0, 3)
+        quantize(1, 0, 0, 2)
+        own_pass(1, 0)
+        own_pass(1, 1)
+        weave(S, 1, 2)
+        weave(S, 1, 3)
+        quantize(1, 1, 0, 1)
+        own_pass(1, 2)
+        finish(0)
+        quantize(1, 1, 1, 2)
+        own_pass(1, 3)
+        finish(1)
+        finish(2)
+        finish(3, 2)

@@ -1,6 +1,7 @@
 from contextlib import ExitStack
 
 import concourse.mybir as mybir
+from concourse.masks import make_identity
 
 K, T, J, N = 1024, 2048, 512, 512
 FLOPS = 2 * 2 * K * N * J
@@ -22,7 +23,7 @@ PACK = 4
 PASSES = 2
 TILES = N // P
 HALF = N // 2
-LIFT = 16
+KB = 1024
 
 
 def tile_list_expert_and_neighbour_kernel(tc, xq_words, xq_scales, wa, wb_words, wb_scales, ga, offs, out):
@@ -32,81 +33,68 @@ def tile_list_expert_and_neighbour_kernel(tc, xq_words, xq_scales, wa, wb_words,
         placed = ctx.enter_context(tc.tile_pool(name="placed", bufs=1))
         psum = ctx.enter_context(tc.psum_pool(name="psum", bufs=1))
 
+        def place(shape, dtype, name, offset):
+            return placed.tile(shape, dtype, name=name, align_bytes=64, offset=offset)
+
         offsets = keep.tile([P, J // 16], U16, name="offsets")
-        blank = placed.tile([P, 3 * P], F32, name="blank", align_bytes=64, offset=7936)
-        xs_table = placed.tile([P, T], U8, name="xs_table", align_bytes=64, offset=11264+0)
-        x_table = [
-            keep.tile([P, T], I32, name="x_table0", align_bytes=64),
-            placed.tile([P, T], I32, name="x_table1", align_bytes=64, offset=0),
-        ]
-        wb_codes = [
-            keep.tile([P, 2 * N], U8, name="wb_codes0", align_bytes=64),
-            placed.tile([P, 2 * N], U8, name="wb_codes1", align_bytes=64, offset=9216),
-        ]
-        x_codes = [
-            placed.tile([P, J], U32, name="x_codes0", align_bytes=64, offset=10240),
-            keep.tile([P, J], U32, name="x_codes1", align_bytes=64),
-        ]
-        wa_raw = placed.tile([P, PASSES * PACK * N], F32, name="wa_raw", align_bytes=64, offset=12288)
-        xs_picked = keep.tile([P, J], U8, name="xs_picked", align_bytes=64)
-        xs_lowered = keep.tile([P, J], U8, name="xs_lowered", align_bytes=64)
-        x_scales = [xs_picked, xs_lowered]
-        wb_planes = placed.tile([P, PASSES, N], U8, name="wb_planes", align_bytes=64, offset=8192)
-        ga_rows = keep.tile([P, PACK], F32, name="ga_rows")
-        ga_wide = placed.tile([P, J], F32, name="ga_wide", align_bytes=64, offset=28672)
+        xs_table = keep.tile([P, PASSES * T], U8, name="xs_table", align_bytes=64)
+        zero = place([P, 5 * KB], F32, "zero", 16 * KB - 64)
+        x_table = [place([P, T], I32, f"x_table{z}", 8 * KB * z) for z in range(PASSES)]
+        x_scales = [keep.tile([P, J], U8, name=f"x_scales{z}", align_bytes=64) for z in range(PASSES)]
+        x_codes = [keep.tile([P, J], U32, name=f"x_codes{z}", align_bytes=64) for z in range(PASSES)]
+        wb_planes = place([P, PASSES, N], U8, "wb_planes", 16 * KB)
+        wb_codes = place([P, PASSES, 2 * N], U8, "wb_codes", 17 * KB)
         identity = keep.tile([P, P], F32, name="identity")
-        zero = keep.tile([P, 1], F32, name="zero")
-        wa_first = wa_raw[:, 0 : PACK * N].rearrange("p (j n) -> p j n", j=PACK)
+        late_zero = place([P, 32], F32, "late_zero", 28 * KB - 64)
+        wa_first = place([P, PACK, N], F32, "wa_first", 20 * KB)
+        wa_rest = place([P, PACK * N], F32, "wa_rest", 28 * KB)
+        ga_rows = keep.tile([P, PACK], F32, name="ga_rows")
         wa_second = [
-            wa_raw[:, PACK * (N + HALF * h) : PACK * (N + HALF * (h + 1))].rearrange("p (j n) -> p j n", j=PACK)
-            for h in range(2)
+            wa_rest[:, PACK * HALF * h : PACK * HALF * (h + 1)].rearrange("p (j n) -> p j n", j=PACK) for h in range(2)
         ]
-        wa_bf = [[keep.tile([P, HALF * PACK], BF16, name=f"wa_bf0{h}", align_bytes=64) for h in range(2)]]
-        wa_bf.append([
-            placed.tile([P, HALF * PACK], BF16, name="wa_bf10", align_bytes=64, offset=28672 + 1024),
-            keep.tile([P, HALF * PACK], BF16, name="wa_bf11", align_bytes=64),
-        ])
+        ga_wide = place([P, J], F32, "ga_wide", 40 * KB)
+        wa_bf = [
+            [keep.tile([P, HALF * PACK], BF16, name=f"wa_bf0{h}", align_bytes=64) for h in range(2)],
+            [place([P, HALF * PACK], BF16, "wa_bf10", 23 * KB), place([P, HALF * PACK], BF16, "wa_bf11", 20 * KB)],
+        ]
+        wa_planes = [
+            [place([P, HALF], U8, f"wa_planes{z}{h}", 40 * KB + HALF * (2 * z + h)) for h in range(2)] for z in range(PASSES)
+        ]
         wa_codes = [[keep.tile([P, HALF], U32, name=f"wa_codes{z}{h}", align_bytes=64) for h in range(2)] for z in range(PASSES)]
-        last_codes = placed.tile([P, P], U32, name="last_codes", align_bytes=64, offset=32768)
-        wa_planes = [[placed.tile([P, HALF], U8, name=f"wa_planes{z}{h}", align_bytes=64, offset=28672 + HALF * (2 * z + h)) for h in range(2)] for z in range(PASSES)]
-        message = [placed.tile([P, J], F32, name=f"message{i}", align_bytes=64, offset=32768 + 4 * J * ((i - 0) % TILES)) for i in range(TILES)]
+        last_codes = place([P, P], U32, "last_codes", 48 * KB)
+        message = [place([P, J], F32, f"message{i}", (48 + 2 * i) * KB) for i in range(TILES)]
         summed = [keep.tile([P, J], F32, name=f"summed{i}") for i in range(TILES)]
         result = [keep.tile([P, J], F32, name=f"result{i}") for i in range(TILES)]
         q_bank = [psum.tile([P, J], F32, name=f"q_bank{i}") for i in range(TILES)]
         p_bank = [psum.tile([P, J], F32, name=f"p_bank{i}") for i in range(TILES)]
 
-        nc.gpsimd.memset(xs_table[:].bitcast(I32), 0)
-        nc.gpsimd.memset(blank[:, 0:P], 0.0)
-        nc.gpsimd.affine_select(
-            out=identity[:], in_=blank[:, 0:P], compare_op=mybir.AluOpType.not_equal, fill=1.0, base=0,
-            pattern=[[-1, P]], channel_multiplier=1,
-        )
-        nc.gpsimd.memset(wb_planes[:].rearrange("p z n -> p (z n)").bitcast(I32), 0)
-        nc.vector.memset(xs_lowered[:].bitcast(I32), 0)
-        nc.vector.memset(zero[:], 0.0)
+        nc.gpsimd.memset(xs_table[:, 0:T].bitcast(I32), 0)
+        nc.vector.memset(xs_table[:, T : PASSES * T].bitcast(I32), 0)
+        nc.gpsimd.memset(zero[:, 0:1], 0.0)
+        make_identity(nc, identity[:])
 
         nc.sync.dma_start(offsets[:], offs)
-        nc.sync.dma_start(x_table[0][:], xq_words[0].rearrange("p t b -> p (t b)").bitcast(I32))
-        nc.sync.dma_start(wb_codes[0][:].bitcast(I32), wb_words[0].bitcast(I32))
         nc.scalar.dma_start(ga_rows[:], ga.rearrange("o (p t) -> (o p) t", t=PACK))
-        xs_rows = xq_scales.rearrange("z (q r) t -> r q z t", r=4)
-        for r in range(4):
-            nc.sync.dma_start(xs_table[r:P:LIFT, :].bitcast(I32), xs_rows[r].bitcast(I32))
+        nc.sync.dma_start(x_table[0][:], xq_words[0].rearrange("p t b -> p (t b)").bitcast(I32))
+        for q in range(4):
+            nc.sync.dma_start(
+                xs_table[32 * q : 32 * q + 4, :].rearrange("p (z t) -> p z t", z=PASSES).bitcast(I32),
+                xq_scales[:, 4 * q : 4 * q + 4, :].rearrange("z r t -> r z t").bitcast(I32),
+            )
+        nc.vector.tensor_copy(message[0][:, 0:1], zero[:, 0:1])
+
         nc.sync.dma_start(x_table[1][:], xq_words[1].rearrange("p t b -> p (t b)").bitcast(I32))
-        nc.sync.dma_start(wb_codes[1][:].bitcast(I32), wb_words[1].bitcast(I32))
+        nc.sync.dma_start(wb_codes[:].bitcast(I32), wb_words.rearrange("z p c -> p z c").bitcast(I32))
+        nc.gpsimd.memset(wb_planes[:].rearrange("p z n -> p (z n)").bitcast(I32), 0)
+        nc.gpsimd.memset(late_zero[:, 0:1], 0.0)
+        for i in range(1, TILES):
+            nc.scalar.activation(message[i][:, 0:1], late_zero[:, 0:1], SILU)
         for q in range(4):
             nc.sync.dma_start(
                 wb_planes[32 * q : 32 * q + 4, :, :].bitcast(I32),
                 wb_scales[:, 4 * q : 4 * q + 4, :].rearrange("z r n -> r z n").bitcast(I32),
             )
-
-        for i in range(TILES):
-            nc.scalar.activation(message[i][:, 0:1], zero[:], SILU)
-
-        nc.vector.tensor_copy(xs_picked[:], xs_table[:].indirect(offsets[:]))
-        nc.sync.dma_start(xs_lowered[0 : P - LIFT, :].bitcast(I32), xs_picked[LIFT:P, :].bitcast(I32))
-        for u in range(2):
-            nc.sync.dma_start(wa_first[:, 2 * u : 2 * u + 2, :], wa[0:512, :].rearrange("(p j) n -> p j n", j=PACK)[:, 2 * u : 2 * u + 2, :])
+        nc.sync.dma_start(wa_first[:], wa[0:512, :].rearrange("(p j) n -> p j n", j=PACK))
         for h in range(2):
             nc.sync.dma_start(
                 wa_second[h], wa[512:1024, h * HALF : (h + 1) * HALF].rearrange("(p j) n -> p j n", j=PACK)
@@ -118,17 +106,25 @@ def tile_list_expert_and_neighbour_kernel(tc, xq_words, xq_scales, wa, wb_words,
         nc.scalar.copy(ga_wide[:].rearrange("n (p t) -> n p t", t=PACK), spread.rearrange("n t p -> n p t"))
 
         for z in range(PASSES):
+            nc.vector.tensor_copy(x_scales[z][:], xs_table[:, T * z : T * (z + 1)].indirect(offsets[:]))
             nc.vector.tensor_copy(x_codes[z][:], x_table[z][:].bitcast(U32).indirect(offsets[:]))
-            for i in range(TILES):
-                nc.tensor.matmul_mx(
-                    out=q_bank[i][:],
-                    lhsT=wb_codes[z][:, 2 * P * i : 2 * P * (i + 1)].bitcast(FP4X4),
-                    lhsT_scale=wb_planes[:, z, P * i : P * (i + 1)],
-                    rhs=x_codes[z][:].bitcast(FP8X4),
-                    rhs_scale=x_scales[z][:],
-                    start=(z == 0),
-                    stop=(z == PASSES - 1),
-                )
+
+        def message_pass(z, i):
+            nc.tensor.matmul_mx(
+                out=q_bank[i][:],
+                lhsT=wb_codes[:, z, 2 * P * i : 2 * P * (i + 1)].bitcast(FP4X4),
+                lhsT_scale=wb_planes[:, z, P * i : P * (i + 1)],
+                rhs=x_codes[z][:].bitcast(FP8X4),
+                rhs_scale=x_scales[z][:],
+                start=(z == 0),
+                stop=(z == PASSES - 1),
+            )
+
+        message_pass(0, 0)
+        for i in range(TILES):
+            if i + 1 < TILES:
+                message_pass(0, i + 1)
+            message_pass(1, i)
 
         def pool_copy(dst, src):
             nc.gpsimd.tensor_scalar(dst, src, 1.0, 0.0, MULT, ADD)
@@ -179,19 +175,20 @@ def tile_list_expert_and_neighbour_kernel(tc, xq_words, xq_scales, wa, wb_words,
         for i in range(TILES):
             weigh(i)
         weave(S, 0, 0, 2)
-        weave(S, 0, 2, 2)
+        weave(G, 0, 2)
+        weave(G, 0, 3)
+        weave(S, 1, 0, 2)
+        weave(S, 1, 2)
+        weave(S, 1, 3)
         quantize(0, 0, 0, 2)
         own_pass(0, 0)
         own_pass(0, 1)
-        weave(V, 1, 0, 2)
         quantize(0, 1, 0, 2)
         own_pass(0, 2)
         own_pass(0, 3)
         quantize(1, 0, 0, 2)
         own_pass(1, 0)
         own_pass(1, 1)
-        weave(S, 1, 2)
-        weave(S, 1, 3)
         quantize(1, 1, 0, 1)
         own_pass(1, 2)
         finish(0)

@@ -38,30 +38,23 @@ def tile_list_expert_and_neighbour_kernel(tc, xq_words, xq_scales, wa, wb_words,
 
         offsets = keep.tile([P, J // 16], U16, name="offsets")
         xs_table = keep.tile([P, PASSES * T], U8, name="xs_table", align_bytes=64)
-        zero = place([P, 5 * KB], F32, "zero", 16 * KB - 64)
+        zero = place([P, 6 * KB], F32, "zero", 16 * KB - 64)
         x_table = [place([P, T], I32, f"x_table{z}", 8 * KB * z) for z in range(PASSES)]
         x_scales = [keep.tile([P, J], U8, name=f"x_scales{z}", align_bytes=64) for z in range(PASSES)]
         x_codes = [keep.tile([P, J], U32, name=f"x_codes{z}", align_bytes=64) for z in range(PASSES)]
         wb_planes = place([P, PASSES, N], U8, "wb_planes", 16 * KB)
         wb_codes = place([P, PASSES, 2 * N], U8, "wb_codes", 17 * KB)
         identity = keep.tile([P, P], F32, name="identity")
-        late_zero = place([P, 32], F32, "late_zero", 28 * KB - 64)
-        wa_first = place([P, PACK, N], F32, "wa_first", 20 * KB)
-        wa_rest = place([P, PACK * N], F32, "wa_rest", 28 * KB)
+        late_zero = place([P, 4 * KB], F32, "late_zero", 20 * KB)
+        wa_first = [place([P, PACK, HALF], F32, f"wa_first{h}", (20 + 4 * h) * KB) for h in range(2)]
+        wa_second = place([P, PACK, N], F32, "wa_second", 28 * KB)
         ga_rows = keep.tile([P, PACK], F32, name="ga_rows")
-        wa_second = [
-            wa_rest[:, PACK * HALF * h : PACK * HALF * (h + 1)].rearrange("p (j n) -> p j n", j=PACK) for h in range(2)
-        ]
         ga_wide = place([P, J], F32, "ga_wide", 40 * KB)
-        wa_bf = [
-            [keep.tile([P, HALF * PACK], BF16, name=f"wa_bf0{h}", align_bytes=64) for h in range(2)],
-            [place([P, HALF * PACK], BF16, "wa_bf10", 23 * KB), place([P, HALF * PACK], BF16, "wa_bf11", 20 * KB)],
-        ]
-        wa_planes = [
-            [place([P, HALF], U8, f"wa_planes{z}{h}", 40 * KB + HALF * (2 * z + h)) for h in range(2)] for z in range(PASSES)
-        ]
-        wa_codes = [[keep.tile([P, HALF], U32, name=f"wa_codes{z}{h}", align_bytes=64) for h in range(2)] for z in range(PASSES)]
-        last_codes = place([P, P], U32, "last_codes", 48 * KB)
+        first_bf = keep.tile([P, N * PACK], BF16, name="first_bf", align_bytes=64)
+        second_bf = [place([P, HALF * PACK], BF16, f"second_bf{h}", (41 + 2 * h) * KB) for h in range(2)]
+        wa_planes = [place([P, N], U8, f"wa_planes{z}", 40 * KB + N * z) for z in range(PASSES)]
+        first_codes = keep.tile([P, N], U32, name="first_codes", align_bytes=64)
+        second_codes = keep.tile([P, N], U32, name="second_codes", align_bytes=64)
         message = [place([P, J], F32, f"message{i}", (48 + 2 * i) * KB) for i in range(TILES)]
         summed = [keep.tile([P, J], F32, name=f"summed{i}") for i in range(TILES)]
         result = [keep.tile([P, J], F32, name=f"result{i}") for i in range(TILES)]
@@ -76,10 +69,10 @@ def tile_list_expert_and_neighbour_kernel(tc, xq_words, xq_scales, wa, wb_words,
         nc.sync.dma_start(offsets[:], offs)
         nc.scalar.dma_start(ga_rows[:], ga.rearrange("o (p t) -> (o p) t", t=PACK))
         nc.sync.dma_start(x_table[0][:], xq_words[0].rearrange("p t b -> p (t b)").bitcast(I32))
-        for q in range(4):
+        xs_rows = xq_scales.rearrange("z (q r) t -> r q z t", r=4)
+        for r in range(4):
             nc.sync.dma_start(
-                xs_table[32 * q : 32 * q + 4, :].rearrange("p (z t) -> p z t", z=PASSES).bitcast(I32),
-                xq_scales[:, 4 * q : 4 * q + 4, :].rearrange("z r t -> r z t").bitcast(I32),
+                xs_table[r:P:32, :].rearrange("p (z t) -> p z t", z=PASSES).bitcast(I32), xs_rows[r].bitcast(I32)
             )
         nc.vector.tensor_copy(message[0][:, 0:1], zero[:, 0:1])
 
@@ -89,25 +82,23 @@ def tile_list_expert_and_neighbour_kernel(tc, xq_words, xq_scales, wa, wb_words,
         nc.gpsimd.memset(late_zero[:, 0:1], 0.0)
         for i in range(1, TILES):
             nc.scalar.activation(message[i][:, 0:1], late_zero[:, 0:1], SILU)
-        for q in range(4):
-            nc.sync.dma_start(
-                wb_planes[32 * q : 32 * q + 4, :, :].bitcast(I32),
-                wb_scales[:, 4 * q : 4 * q + 4, :].rearrange("z r n -> r z n").bitcast(I32),
-            )
-        nc.sync.dma_start(wa_first[:], wa[0:512, :].rearrange("(p j) n -> p j n", j=PACK))
+        wb_rows = wb_scales.rearrange("z (q r) n -> r q z n", r=4)
+        for r in range(4):
+            nc.sync.dma_start(wb_planes[r:P:32, :, :].bitcast(I32), wb_rows[r].bitcast(I32))
+        wa_rows = wa.rearrange("(z p j) n -> z p j n", z=PASSES, j=PACK)
         for h in range(2):
-            nc.sync.dma_start(
-                wa_second[h], wa[512:1024, h * HALF : (h + 1) * HALF].rearrange("(p j) n -> p j n", j=PACK)
-            )
+            nc.sync.dma_start(wa_first[h][:], wa_rows[0][:, :, h * HALF : (h + 1) * HALF])
+        nc.sync.dma_start(wa_second[:], wa_rows[1])
+
+        for z in range(PASSES):
+            nc.vector.tensor_copy(x_codes[z][:] if z == 0 else x_scales[0][:], (x_table[0][:].bitcast(U32) if z == 0 else xs_table[:, 0:T]).indirect(offsets[:]))
+        nc.vector.tensor_copy(x_scales[1][:], xs_table[:, T : 2 * T].indirect(offsets[:]))
+        nc.vector.tensor_copy(x_codes[1][:], x_table[1][:].bitcast(U32).indirect(offsets[:]))
 
         spread = p_bank[TILES - 1][:].rearrange("n (t p) -> n t p", t=PACK)
         for t in range(PACK):
             nc.tensor.transpose(spread[:, t, :], ga_rows[:, t : t + 1].to_broadcast([P, P]), identity[:])
         nc.scalar.copy(ga_wide[:].rearrange("n (p t) -> n p t", t=PACK), spread.rearrange("n t p -> n p t"))
-
-        for z in range(PASSES):
-            nc.vector.tensor_copy(x_scales[z][:], xs_table[:, T * z : T * (z + 1)].indirect(offsets[:]))
-            nc.vector.tensor_copy(x_codes[z][:], x_table[z][:].bitcast(U32).indirect(offsets[:]))
 
         def message_pass(z, i):
             nc.tensor.matmul_mx(
@@ -126,35 +117,38 @@ def tile_list_expert_and_neighbour_kernel(tc, xq_words, xq_scales, wa, wb_words,
                 message_pass(0, i + 1)
             message_pass(1, i)
 
-        def pool_copy(dst, src):
-            nc.gpsimd.tensor_scalar(dst, src, 1.0, 0.0, MULT, ADD)
+        S, V = nc.scalar.copy, nc.vector.tensor_copy
 
-        S, V, G = nc.scalar.copy, nc.vector.tensor_copy, pool_copy
+        def staged(z, i, count):
+            if z == 0:
+                return first_bf[:, PACK * P * i : PACK * P * (i + count)]
+            return second_bf[i // 2][:, PACK * P * (i % 2) : PACK * P * (i % 2 + count)]
 
         def weave(engine_copy, z, i, count=1):
-            h, c = divmod(i, 2)
-            rows = wa_first[:, :, P * i : P * (i + count)] if z == 0 else wa_second[h][:, :, P * c : P * (c + count)]
-            dst = wa_bf[z][h][:, PACK * P * c : PACK * P * (c + count)]
+            if z == 0:
+                rows = wa_first[i // 2][:, :, P * (i % 2) : P * (i % 2 + count)]
+            else:
+                rows = wa_second[:, :, P * i : P * (i + count)]
             engine_copy(
-                dst.rearrange("p (c i t) -> p c t i", i=4, t=PACK), rows.rearrange("p t (c i) -> p c t i", i=4)
+                staged(z, i, count).rearrange("p (c i t) -> p c t i", i=4, t=PACK),
+                rows.rearrange("p t (c i) -> p c t i", i=4),
             )
 
-        def codes(z, h, c0, c1):
-            return last_codes[:] if (z, h, c0) == (1, 1, 1) else wa_codes[z][h][:, P * c0 : P * c1]
+        def codes(z, i, count=1):
+            return (first_codes if z == 0 else second_codes)[:, P * i : P * (i + count)]
 
-        def quantize(z, h, c0, c1):
+        def quantize(z, i, count=1):
             nc.vector.quantize_mx(
-                out=codes(z, h, c0, c1).bitcast(FP8X4),
-                scales=wa_planes[z][h][:, P * c0 : P * c1],
-                in_=wa_bf[z][h][:, PACK * P * c0 : PACK * P * c1],
+                out=codes(z, i, count).bitcast(FP8X4),
+                scales=wa_planes[z][:, P * i : P * (i + count)],
+                in_=staged(z, i, count),
             )
 
         def own_pass(z, i):
-            h, c = divmod(i, 2)
             nc.tensor.matmul_mx(
                 out=p_bank[i][:],
-                lhsT=codes(z, h, c, c + 1).bitcast(FP8X4),
-                lhsT_scale=wa_planes[z][h][:, P * c : P * (c + 1)],
+                lhsT=codes(z, i).bitcast(FP8X4),
+                lhsT_scale=wa_planes[z][:, P * i : P * (i + 1)],
                 rhs=x_codes[z][:].bitcast(FP8X4),
                 rhs_scale=x_scales[z][:],
                 start=(z == 0),
@@ -175,25 +169,24 @@ def tile_list_expert_and_neighbour_kernel(tc, xq_words, xq_scales, wa, wb_words,
         for i in range(TILES):
             weigh(i)
         weave(S, 0, 0, 2)
-        weave(G, 0, 2)
-        weave(G, 0, 3)
-        weave(S, 1, 0, 2)
-        weave(S, 1, 2)
-        weave(S, 1, 3)
-        quantize(0, 0, 0, 2)
+        weave(S, 0, 2, 2)
+        weave(S, 1, 2, 2)
+        quantize(0, 0, 2)
         own_pass(0, 0)
         own_pass(0, 1)
-        quantize(0, 1, 0, 2)
+        quantize(0, 2, 2)
         own_pass(0, 2)
         own_pass(0, 3)
-        quantize(1, 0, 0, 2)
+        weave(V, 1, 0)
+        weave(V, 1, 1)
+        quantize(1, 0)
         own_pass(1, 0)
+        quantize(1, 1)
         own_pass(1, 1)
-        quantize(1, 1, 0, 1)
+        quantize(1, 2, 2)
         own_pass(1, 2)
-        finish(0)
-        quantize(1, 1, 1, 2)
         own_pass(1, 3)
+        finish(0)
         finish(1)
         finish(2)
         finish(3, 2)

@@ -20,10 +20,20 @@ SILU = mybir.ActivationFunctionType.Silu
 
 P = 128
 PACK = 4
-PASSES = 2
+PASSES = K // (P * PACK)
 TILES = N // P
 HALF = N // 2
+QUADRANT = 32
+SCALE_ROWS = 4
+LINE = 4
 KB = 1024
+
+X_TABLES_AT = 0
+WB_PLANES_AT = 16 * KB
+WB_CODES_AT = 17 * KB
+WA_AT = 20 * KB
+GA_AT = 40 * KB
+MESSAGES_AT = 48 * KB
 
 
 def tile_list_expert_and_neighbour_kernel(tc, xq_words, xq_scales, wa, wb_words, wb_scales, ga, offs, out):
@@ -38,24 +48,25 @@ def tile_list_expert_and_neighbour_kernel(tc, xq_words, xq_scales, wa, wb_words,
 
         offsets = keep.tile([P, J // 16], U16, name="offsets")
         xs_table = keep.tile([P, PASSES * T], U8, name="xs_table", align_bytes=64)
-        zero = place([P, 6 * KB], F32, "zero", 16 * KB - 64)
-        x_table = [place([P, T], I32, f"x_table{z}", 8 * KB * z) for z in range(PASSES)]
+        zero = place([P, 6 * KB], F32, "zero", WB_PLANES_AT - 64)
+        x_table = [place([P, T], I32, f"x_table{z}", X_TABLES_AT + 4 * T * z) for z in range(PASSES)]
         x_scales = [keep.tile([P, J], U8, name=f"x_scales{z}", align_bytes=64) for z in range(PASSES)]
         x_codes = [keep.tile([P, J], U32, name=f"x_codes{z}", align_bytes=64) for z in range(PASSES)]
-        wb_planes = place([P, PASSES, N], U8, "wb_planes", 16 * KB)
-        wb_codes = place([P, PASSES, 2 * N], U8, "wb_codes", 17 * KB)
+        wb_planes = place([P, PASSES, N], U8, "wb_planes", WB_PLANES_AT)
+        wb_codes = place([P, PASSES, 2 * N], U8, "wb_codes", WB_CODES_AT)
         identity = keep.tile([P, P], F32, name="identity")
-        late_zero = place([P, 4 * KB], F32, "late_zero", 20 * KB)
-        wa_first = [place([P, PACK, HALF], F32, f"wa_first{h}", (20 + 4 * h) * KB) for h in range(2)]
-        wa_second = place([P, PACK, N], F32, "wa_second", 28 * KB)
+        late_zero = place([P, 4 * KB], F32, "late_zero", WA_AT)
+        wa_first = [place([P, PACK, HALF], F32, f"wa_first{h}", WA_AT + 4 * PACK * HALF * h) for h in range(2)]
+        wa_second = place([P, PACK, N], F32, "wa_second", WA_AT + 4 * PACK * N)
         ga_rows = keep.tile([P, PACK], F32, name="ga_rows")
-        ga_wide = place([P, J], F32, "ga_wide", 40 * KB)
+        ga_wide = place([P, J], F32, "ga_wide", GA_AT)
         first_bf = keep.tile([P, N * PACK], BF16, name="first_bf", align_bytes=64)
-        second_bf = [place([P, HALF * PACK], BF16, f"second_bf{h}", (41 + 2 * h) * KB) for h in range(2)]
-        wa_planes = [place([P, N], U8, f"wa_planes{z}", 40 * KB + N * z) for z in range(PASSES)]
+        second_bf = [place([P, P * PACK], BF16, f"second_bf{i}", GA_AT + KB + 2 * P * PACK * i) for i in range(TILES)]
+        wa_planes = [place([P, N], U8, f"wa_planes{z}", GA_AT + N * z) for z in range(PASSES)]
         first_codes = keep.tile([P, N], U32, name="first_codes", align_bytes=64)
-        second_codes = keep.tile([P, N], U32, name="second_codes", align_bytes=64)
-        message = [place([P, J], F32, f"message{i}", (48 + 2 * i) * KB) for i in range(TILES)]
+        second_codes = [keep.tile([P, P], U32, name=f"second_codes{i}", align_bytes=64) for i in range(TILES - 1)]
+        second_codes.append(place([P, P], U32, "last_codes", MESSAGES_AT))
+        message = [place([P, J], F32, f"message{i}", MESSAGES_AT + 4 * J * i) for i in range(TILES)]
         summed = [keep.tile([P, J], F32, name=f"summed{i}") for i in range(TILES)]
         result = [keep.tile([P, J], F32, name=f"result{i}") for i in range(TILES)]
         q_bank = [psum.tile([P, J], F32, name=f"q_bank{i}") for i in range(TILES)]
@@ -69,10 +80,10 @@ def tile_list_expert_and_neighbour_kernel(tc, xq_words, xq_scales, wa, wb_words,
         nc.sync.dma_start(offsets[:], offs)
         nc.scalar.dma_start(ga_rows[:], ga.rearrange("o (p t) -> (o p) t", t=PACK))
         nc.sync.dma_start(x_table[0][:], xq_words[0].rearrange("p t b -> p (t b)").bitcast(I32))
-        xs_rows = xq_scales.rearrange("z (q r) t -> r q z t", r=4)
-        for r in range(4):
+        xs_rows = xq_scales.rearrange("z (q r) t -> r q z t", r=SCALE_ROWS)
+        for r in range(SCALE_ROWS):
             nc.sync.dma_start(
-                xs_table[r:P:32, :].rearrange("p (z t) -> p z t", z=PASSES).bitcast(I32), xs_rows[r].bitcast(I32)
+                xs_table[r:P:QUADRANT, :].rearrange("p (z t) -> p z t", z=PASSES).bitcast(I32), xs_rows[r].bitcast(I32)
             )
         nc.vector.tensor_copy(message[0][:, 0:1], zero[:, 0:1])
 
@@ -82,17 +93,17 @@ def tile_list_expert_and_neighbour_kernel(tc, xq_words, xq_scales, wa, wb_words,
         nc.gpsimd.memset(late_zero[:, 0:1], 0.0)
         for i in range(1, TILES):
             nc.scalar.activation(message[i][:, 0:1], late_zero[:, 0:1], SILU)
-        wb_rows = wb_scales.rearrange("z (q r) n -> r q z n", r=4)
-        for r in range(4):
-            nc.sync.dma_start(wb_planes[r:P:32, :, :].bitcast(I32), wb_rows[r].bitcast(I32))
-        wa_rows = wa.rearrange("(z p j) n -> z p j n", z=PASSES, j=PACK)
+        wb_rows = wb_scales.rearrange("z (q r) n -> r q z n", r=SCALE_ROWS)
+        for r in range(SCALE_ROWS):
+            nc.sync.dma_start(wb_planes[r:P:QUADRANT, :, :].bitcast(I32), wb_rows[r].bitcast(I32))
+        wa_rows = wa.rearrange("(z p t) n -> z p t n", z=PASSES, t=PACK)
         for h in range(2):
             nc.sync.dma_start(wa_first[h][:], wa_rows[0][:, :, h * HALF : (h + 1) * HALF])
         nc.sync.dma_start(wa_second[:], wa_rows[1])
 
+        nc.vector.tensor_copy(x_codes[0][:], x_table[0][:].bitcast(U32).indirect(offsets[:]))
         for z in range(PASSES):
-            nc.vector.tensor_copy(x_codes[z][:] if z == 0 else x_scales[0][:], (x_table[0][:].bitcast(U32) if z == 0 else xs_table[:, 0:T]).indirect(offsets[:]))
-        nc.vector.tensor_copy(x_scales[1][:], xs_table[:, T : 2 * T].indirect(offsets[:]))
+            nc.vector.tensor_copy(x_scales[z][:], xs_table[:, T * z : T * (z + 1)].indirect(offsets[:]))
         nc.vector.tensor_copy(x_codes[1][:], x_table[1][:].bitcast(U32).indirect(offsets[:]))
 
         spread = p_bank[TILES - 1][:].rearrange("n (t p) -> n t p", t=PACK)
@@ -117,76 +128,63 @@ def tile_list_expert_and_neighbour_kernel(tc, xq_words, xq_scales, wa, wb_words,
                 message_pass(0, i + 1)
             message_pass(1, i)
 
-        S, V = nc.scalar.copy, nc.vector.tensor_copy
-
         def staged(z, i, count):
             if z == 0:
                 return first_bf[:, PACK * P * i : PACK * P * (i + count)]
-            return second_bf[i // 2][:, PACK * P * (i % 2) : PACK * P * (i % 2 + count)]
+            return second_bf[i][:]
 
-        def weave(engine_copy, z, i, count=1):
+        def cast(engine_copy, z, i, count=1):
             if z == 0:
                 rows = wa_first[i // 2][:, :, P * (i % 2) : P * (i % 2 + count)]
             else:
                 rows = wa_second[:, :, P * i : P * (i + count)]
             engine_copy(
-                staged(z, i, count).rearrange("p (c i t) -> p c t i", i=4, t=PACK),
-                rows.rearrange("p t (c i) -> p c t i", i=4),
+                staged(z, i, count).rearrange("p (c e t) -> p c t e", e=LINE, t=PACK),
+                rows.rearrange("p t (c e) -> p c t e", e=LINE),
             )
 
         def codes(z, i, count=1):
-            return (first_codes if z == 0 else second_codes)[:, P * i : P * (i + count)]
+            return first_codes[:, P * i : P * (i + count)] if z == 0 else second_codes[i][:]
 
-        def quantize(z, i, count=1):
+        def own_passes(z, first, count=1):
             nc.vector.quantize_mx(
-                out=codes(z, i, count).bitcast(FP8X4),
-                scales=wa_planes[z][:, P * i : P * (i + count)],
-                in_=staged(z, i, count),
+                out=codes(z, first, count).bitcast(FP8X4),
+                scales=wa_planes[z][:, P * first : P * (first + count)],
+                in_=staged(z, first, count),
             )
-
-        def own_pass(z, i):
-            nc.tensor.matmul_mx(
-                out=p_bank[i][:],
-                lhsT=codes(z, i).bitcast(FP8X4),
-                lhsT_scale=wa_planes[z][:, P * i : P * (i + 1)],
-                rhs=x_codes[z][:].bitcast(FP8X4),
-                rhs_scale=x_scales[z][:],
-                start=(z == 0),
-                stop=(z == PASSES - 1),
-            )
-
-        def weigh(i):
-            nc.vector.tensor_tensor(message[i][:, 1:J], q_bank[i][:, 0 : J - 1], ga_wide[:, 1:J], MULT)
+            for i in range(first, first + count):
+                nc.tensor.matmul_mx(
+                    out=p_bank[i][:],
+                    lhsT=codes(z, i).bitcast(FP8X4),
+                    lhsT_scale=wa_planes[z][:, P * i : P * (i + 1)],
+                    rhs=x_codes[z][:].bitcast(FP8X4),
+                    rhs_scale=x_scales[z][:],
+                    start=(z == 0),
+                    stop=(z == PASSES - 1),
+                )
 
         def finish(i, parts=1):
-            w = J // parts
+            width = J // parts
             for s in range(parts):
-                cols = slice(w * s, w * (s + 1))
+                cols = slice(width * s, width * (s + 1))
                 nc.vector.tensor_tensor(summed[i][:, cols], p_bank[i][:, cols], message[i][:, cols], ADD)
                 nc.scalar.activation(result[i][:, cols], summed[i][:, cols], SILU)
                 nc.sync.dma_start(out[P * i : P * (i + 1), cols], result[i][:, cols])
 
         for i in range(TILES):
-            weigh(i)
-        weave(S, 0, 0, 2)
-        weave(S, 0, 2, 2)
-        weave(S, 1, 2, 2)
-        quantize(0, 0, 2)
-        own_pass(0, 0)
-        own_pass(0, 1)
-        quantize(0, 2, 2)
-        own_pass(0, 2)
-        own_pass(0, 3)
-        weave(V, 1, 0)
-        weave(V, 1, 1)
-        quantize(1, 0)
-        own_pass(1, 0)
-        quantize(1, 1)
-        own_pass(1, 1)
-        quantize(1, 2, 2)
-        own_pass(1, 2)
-        own_pass(1, 3)
+            nc.vector.tensor_tensor(message[i][:, 1:J], q_bank[i][:, 0 : J - 1], ga_wide[:, 1:J], MULT)
+
+        for h in range(2):
+            cast(nc.scalar.copy, 0, 2 * h, 2)
+        for i in range(1, TILES):
+            cast(nc.scalar.copy, 1, i)
+        for h in range(2):
+            own_passes(0, 2 * h, 2)
+        cast(nc.vector.tensor_copy, 1, 0)
+        for i in range(TILES - 1):
+            own_passes(1, i)
         finish(0)
-        finish(1)
-        finish(2)
-        finish(3, 2)
+        own_passes(1, TILES - 1)
+        for i in range(1, TILES - 1):
+            finish(i)
+        finish(TILES - 1, parts=2)

from contextlib import ExitStack

import concourse.mybir as mybir
from concourse.masks import make_identity

K, T, J, N = 1024, 2048, 512, 512
FLOPS = 2 * 2 * K * N * J

F32 = mybir.dt.float32
BF16 = mybir.dt.bfloat16
I32 = mybir.dt.int32
U32 = mybir.dt.uint32
U16 = mybir.dt.uint16
U8 = mybir.dt.uint8
FP8X4 = mybir.dt.float8_e4m3fn_x4
FP4X4 = mybir.dt.float4_e2m1fn_x4
MULT = mybir.AluOpType.mult
ADD = mybir.AluOpType.add
SILU = mybir.ActivationFunctionType.Silu

P = 128
PACK = 4
PASSES = K // (P * PACK)
TILES = N // P
HALF = N // 2
QUADRANT = 32
SCALE_ROWS = 4
LINE = 4
KB = 1024

X_TABLES_AT = 0
WB_PLANES_AT = 16 * KB
WB_CODES_AT = 17 * KB
WA_AT = 20 * KB
GA_AT = 40 * KB
MESSAGES_AT = 48 * KB


def tile_list_expert_and_neighbour_kernel(tc, xq_words, xq_scales, wa, wb_words, wb_scales, ga, offs, out):
    nc = tc.nc
    with ExitStack() as ctx:
        keep = ctx.enter_context(tc.tile_pool(name="keep", bufs=1))
        placed = ctx.enter_context(tc.tile_pool(name="placed", bufs=1))
        psum = ctx.enter_context(tc.psum_pool(name="psum", bufs=1))

        def place(shape, dtype, name, offset):
            return placed.tile(shape, dtype, name=name, align_bytes=64, offset=offset)

        offsets = keep.tile([P, J // 16], U16, name="offsets")
        xs_table = keep.tile([P, PASSES * T], U8, name="xs_table", align_bytes=64)
        zero = place([P, 6 * KB], F32, "zero", WB_PLANES_AT - 64)
        x_table = [place([P, T], I32, f"x_table{z}", X_TABLES_AT + 4 * T * z) for z in range(PASSES)]
        x_scales = [keep.tile([P, J], U8, name=f"x_scales{z}", align_bytes=64) for z in range(PASSES)]
        x_codes = [keep.tile([P, J], U32, name=f"x_codes{z}", align_bytes=64) for z in range(PASSES)]
        wb_planes = place([P, PASSES, N], U8, "wb_planes", WB_PLANES_AT)
        wb_codes = place([P, PASSES, 2 * N], U8, "wb_codes", WB_CODES_AT)
        identity = keep.tile([P, P], F32, name="identity")
        late_zero = place([P, 4 * KB], F32, "late_zero", WA_AT)
        wa_first = [place([P, PACK, HALF], F32, f"wa_first{h}", WA_AT + 4 * PACK * HALF * h) for h in range(2)]
        wa_second = place([P, PACK, N], F32, "wa_second", WA_AT + 4 * PACK * N)
        ga_rows = keep.tile([P, PACK], F32, name="ga_rows")
        ga_wide = place([P, J], F32, "ga_wide", GA_AT)
        first_bf = keep.tile([P, N * PACK], BF16, name="first_bf", align_bytes=64)
        second_bf = [place([P, P * PACK], BF16, f"second_bf{i}", GA_AT + KB + 2 * P * PACK * i) for i in range(TILES)]
        wa_planes = [place([P, N], U8, f"wa_planes{z}", GA_AT + N * z) for z in range(PASSES)]
        first_codes = keep.tile([P, N], U32, name="first_codes", align_bytes=64)
        second_codes = [keep.tile([P, P], U32, name=f"second_codes{i}", align_bytes=64) for i in range(TILES - 1)]
        second_codes.append(place([P, P], U32, "last_codes", MESSAGES_AT))
        message = [place([P, J], F32, f"message{i}", MESSAGES_AT + 4 * J * i) for i in range(TILES)]
        summed = [keep.tile([P, J], F32, name=f"summed{i}") for i in range(TILES)]
        result = [keep.tile([P, J], F32, name=f"result{i}") for i in range(TILES)]
        q_bank = [psum.tile([P, J], F32, name=f"q_bank{i}") for i in range(TILES)]
        p_bank = [psum.tile([P, J], F32, name=f"p_bank{i}") for i in range(TILES)]

        nc.gpsimd.memset(xs_table[:, 0:T].bitcast(I32), 0)
        nc.vector.memset(xs_table[:, T : PASSES * T].bitcast(I32), 0)
        nc.gpsimd.memset(zero[:, 0:1], 0.0)
        make_identity(nc, identity[:])

        nc.sync.dma_start(offsets[:], offs)
        nc.scalar.dma_start(ga_rows[:], ga.rearrange("o (p t) -> (o p) t", t=PACK))
        nc.sync.dma_start(x_table[0][:], xq_words[0].rearrange("p t b -> p (t b)").bitcast(I32))
        xs_rows = xq_scales.rearrange("z (q r) t -> r q z t", r=SCALE_ROWS)
        for r in range(SCALE_ROWS):
            nc.sync.dma_start(
                xs_table[r:P:QUADRANT, :].rearrange("p (z t) -> p z t", z=PASSES).bitcast(I32), xs_rows[r].bitcast(I32)
            )
        nc.vector.tensor_copy(message[0][:, 0:1], zero[:, 0:1])

        nc.sync.dma_start(x_table[1][:], xq_words[1].rearrange("p t b -> p (t b)").bitcast(I32))
        nc.sync.dma_start(wb_codes[:].bitcast(I32), wb_words.rearrange("z p c -> p z c").bitcast(I32))
        nc.gpsimd.memset(wb_planes[:].rearrange("p z n -> p (z n)").bitcast(I32), 0)
        nc.gpsimd.memset(late_zero[:, 0:1], 0.0)
        for i in range(1, TILES):
            nc.scalar.activation(message[i][:, 0:1], late_zero[:, 0:1], SILU)
        wb_rows = wb_scales.rearrange("z (q r) n -> r q z n", r=SCALE_ROWS)
        for r in range(SCALE_ROWS):
            nc.sync.dma_start(wb_planes[r:P:QUADRANT, :, :].bitcast(I32), wb_rows[r].bitcast(I32))
        wa_rows = wa.rearrange("(z p t) n -> z p t n", z=PASSES, t=PACK)
        for h in range(2):
            nc.sync.dma_start(wa_first[h][:], wa_rows[0][:, :, h * HALF : (h + 1) * HALF])
        nc.sync.dma_start(wa_second[:], wa_rows[1])

        nc.vector.tensor_copy(x_codes[0][:], x_table[0][:].bitcast(U32).indirect(offsets[:]))
        for z in range(PASSES):
            nc.vector.tensor_copy(x_scales[z][:], xs_table[:, T * z : T * (z + 1)].indirect(offsets[:]))
        nc.vector.tensor_copy(x_codes[1][:], x_table[1][:].bitcast(U32).indirect(offsets[:]))

        spread = p_bank[TILES - 1][:].rearrange("n (t p) -> n t p", t=PACK)
        for t in range(PACK):
            nc.tensor.transpose(spread[:, t, :], ga_rows[:, t : t + 1].to_broadcast([P, P]), identity[:])
        nc.scalar.copy(ga_wide[:].rearrange("n (p t) -> n p t", t=PACK), spread.rearrange("n t p -> n p t"))

        def message_pass(z, i):
            nc.tensor.matmul_mx(
                out=q_bank[i][:],
                lhsT=wb_codes[:, z, 2 * P * i : 2 * P * (i + 1)].bitcast(FP4X4),
                lhsT_scale=wb_planes[:, z, P * i : P * (i + 1)],
                rhs=x_codes[z][:].bitcast(FP8X4),
                rhs_scale=x_scales[z][:],
                start=(z == 0),
                stop=(z == PASSES - 1),
            )

        message_pass(0, 0)
        for i in range(TILES):
            if i + 1 < TILES:
                message_pass(0, i + 1)
            message_pass(1, i)

        def staged(z, i, count):
            if z == 0:
                return first_bf[:, PACK * P * i : PACK * P * (i + count)]
            return second_bf[i][:]

        def cast(engine_copy, z, i, count=1):
            if z == 0:
                rows = wa_first[i // 2][:, :, P * (i % 2) : P * (i % 2 + count)]
            else:
                rows = wa_second[:, :, P * i : P * (i + count)]
            engine_copy(
                staged(z, i, count).rearrange("p (c e t) -> p c t e", e=LINE, t=PACK),
                rows.rearrange("p t (c e) -> p c t e", e=LINE),
            )

        def codes(z, i, count=1):
            return first_codes[:, P * i : P * (i + count)] if z == 0 else second_codes[i][:]

        def own_passes(z, first, count=1):
            nc.vector.quantize_mx(
                out=codes(z, first, count).bitcast(FP8X4),
                scales=wa_planes[z][:, P * first : P * (first + count)],
                in_=staged(z, first, count),
            )
            for i in range(first, first + count):
                nc.tensor.matmul_mx(
                    out=p_bank[i][:],
                    lhsT=codes(z, i).bitcast(FP8X4),
                    lhsT_scale=wa_planes[z][:, P * i : P * (i + 1)],
                    rhs=x_codes[z][:].bitcast(FP8X4),
                    rhs_scale=x_scales[z][:],
                    start=(z == 0),
                    stop=(z == PASSES - 1),
                )

        def finish(i, parts=1):
            width = J // parts
            for s in range(parts):
                cols = slice(width * s, width * (s + 1))
                nc.vector.tensor_tensor(summed[i][:, cols], p_bank[i][:, cols], message[i][:, cols], ADD)
                nc.scalar.activation(result[i][:, cols], summed[i][:, cols], SILU)
                nc.sync.dma_start(out[P * i : P * (i + 1), cols], result[i][:, cols])

        for i in range(TILES):
            nc.vector.tensor_tensor(message[i][:, 1:J], q_bank[i][:, 0 : J - 1], ga_wide[:, 1:J], MULT)

        for h in range(2):
            cast(nc.scalar.copy, 0, 2 * h, 2)
        for i in range(1, TILES):
            cast(nc.scalar.copy, 1, i)
        for h in range(2):
            own_passes(0, 2 * h, 2)
        cast(nc.vector.tensor_copy, 1, 0)
        for i in range(TILES - 1):
            own_passes(1, i)
        finish(0)
        own_passes(1, TILES - 1)
        for i in range(1, TILES - 1):
            finish(i)
        finish(TILES - 1, parts=2)
